import numpy as np, ml_dtypes
CORES = [6,15,38,47]
N = 4
import mx_ref
BF = ml_dtypes.bfloat16
def entries(a):
    return np.ascontiguousarray(a.T).reshape(-1)
def table(e):
    return np.ascontiguousarray(np.reshape(e, (-1, 16)).T).astype(np.int32)
def cols(t, e):
    v = np.concatenate([t.reshape(128, -1, 4), np.zeros((128, 1, 4), BF)], axis=1)
    return np.ascontiguousarray(v[:, e]).reshape(128, -1)
def tile(rs):
    return np.stack(rs, axis=2).reshape(128, -1).astype(BF)
def cut(t, i, w=512):
    return t[:, w * i:w * i + w]
def f(rng, *shape):
    return mx_ref.flush((rng.standard_normal(shape, dtype=np.float32) * np.exp2(rng.integers(-2, 3, shape[:-1] + (1,)))).astype(BF))
def wide(rng, *shape, cols=0):
    v = rng.standard_normal(shape, dtype=np.float32) * np.exp2(rng.integers(-12, 13, shape)).astype(np.float32)
    if cols: v *= np.repeat(np.exp2(rng.integers(-cols, cols + 1, shape[:-2] + (1, shape[-1] // 4))) * (rng.random(shape[:-2] + (1, shape[-1] // 4)) > 0.0625), 4, axis=-1).astype(np.float32)
    return mx_ref.flush(v.astype(BF))
T, E, CN, CM = 256, 512, 128, 144
def lists(rng, popular=False, lonely=False, far=False):
    n, m = np.full((N, N, CN), -1), np.full((N, N, CM), -1)
    for q in range(N):
        for d in range(N):
            if d != q:
                k = rng.permutation(CN)[:CN if far else rng.integers(CN // 2, CN + 1)]; n[q, d, k] = rng.integers(0, T, len(k))
            k = rng.permutation(CM)[:CM if far else rng.integers(CM // 2, CM + 1)]; m[q, d, k] = 0
        u = m[q] == 0
        m[q][u] = rng.permutation(np.resize(rng.permutation(E), int(u.sum())))
    es, ed, nl = [], [], []
    for r in range(N):
        u = T + np.flatnonzero(n[:, r].reshape(-1) >= 0)
        if far: h = rng.permutation(np.resize(rng.permutation(u), 2 * E))
        else: h = rng.choice(np.concatenate([np.arange(T), u]), 2 * E)
        a, b = h[:E].copy(), h[E:].copy()
        if popular: a[rng.permutation(E)[:3 * E // 4]] = rng.choice(u)
        es.append(table(a)); ed.append(table(b))
        w = np.flatnonzero(m[:, r].reshape(-1) >= 0)
        j = rng.permutation(T)[:T // 2 if lonely else T]
        p = (4 * j[:, None] + rng.permuted(np.tile(np.arange(4), (len(j), 1)), axis=1)).T.reshape(-1)
        if not lonely: p = rng.permutation(p)
        k = len(p) if far else min(len(p), len(w) + int(rng.integers(0, T)))
        t = np.full(4 * T, -1); t[p[:k]] = rng.permutation(np.resize(rng.permutation(w), k))
        nl.append(table(t))
    return {"sn": np.stack([table(n[q].reshape(-1)) for q in range(N)]), "es": np.stack(es), "ed": np.stack(ed), "sm": np.stack([table(m[q].reshape(-1)) for q in range(N)]), "nl": np.stack(nl)}
def setup_inputs(rng):
    return {"x": f(rng, N, 128, 4 * T), "e": f(rng, N, 128, 4 * E), "wa": np.repeat(f(rng, 1, 128, 2048), N, axis=0), "wb": np.repeat(f(rng, 1, 128, 2048), N, axis=0), "v": f(rng, N, 128, 512), **lists(rng)}
def setup_inputs_popular(rng):
    return {**setup_inputs(rng), **lists(rng, popular=True)}
def setup_inputs_lonely(rng):
    d = {**setup_inputs(rng), **lists(rng, lonely=True)}; d["v"] = (d["v"].astype(np.float32) * np.float32(2.0 ** 24)).astype(BF); d["e"] = (d["e"].astype(np.float32) * np.float32(2.0 ** 20)).astype(BF); return d
def setup_inputs_far(rng):
    return {**setup_inputs(rng), **lists(rng, far=True)}
def setup_inputs_cancel(rng):
    d = setup_inputs(rng); d["wb"] = -d["wa"]
    for r in range(N):
        a, b = entries(d["es"][r]), entries(d["ed"][r]).copy()
        k = rng.permutation(E)[:3 * E // 4]; b[k] = a[k]; d["ed"][r] = table(b)
    d["e"] = mx_ref.flush((d["e"].astype(np.float32) * np.float32(2.0 ** -10)).astype(BF)); return d
def setup_inputs_spread(rng):
    d = setup_inputs(rng); d["x"] = wide(rng, N, 128, 4 * T, cols=4); d["e"] = wide(rng, N, 128, 4 * E, cols=4); return d
def check_inputs(d):
    b = []
    for k in ("wa", "wb"):
        if (d[k] != d[k][:1]).any(): b.append(k)
    n = [entries(d["sn"][q]).reshape(N, CN) for q in range(N)]; m = [entries(d["sm"][q]).reshape(N, CM) for q in range(N)]
    for r in range(N):
        if n[r].min() < -1 or n[r].max() >= T or (n[r][r] != -1).any(): b.append("sn")
        if m[r].min() < -1 or m[r].max() >= E: b.append("sm")
        ok = np.concatenate([np.ones(T, bool)] + [n[q][r] >= 0 for q in range(N)])
        for k in ("es", "ed"):
            h = entries(d[k][r])
            if h.min() < 0 or h.max() >= T + N * CN or not ok[h].all(): b.append(k)
        ok = np.concatenate([m[q][r] >= 0 for q in range(N)]); h = entries(d["nl"][r])
        if h.min() < -1 or h.max() >= N * CM or not ok[h[h >= 0]].all(): b.append("nl")
    return b
def reference(x, e, wa, wb, v, sn, es, ed, sm, nl):
    M = []
    for r in range(N):
        X = np.concatenate([x[r]] + [cols(x[q], entries(sn[q])[r * CN:r * CN + CN]) for q in range(N)], axis=1)
        src, dst = mx_ref.quantize(cols(X, entries(es[r]))), mx_ref.quantize(cols(X, entries(ed[r])))
        rs = []
        for i in range(4):
            a = mx_ref.matmul(mx_ref.quantize(np.ascontiguousarray(cut(wa[r], i))), src)
            b = mx_ref.matmul(mx_ref.quantize(np.ascontiguousarray(cut(wb[r], i))), dst)
            rs.append(np.maximum((a + b) + e[r][:, i::4].astype(np.float32), np.float32(0)) * np.float32(0.05))
        M.append(tile(rs))
    y = np.zeros((N, 128, T), np.float32)
    for r in range(N):
        P = mx_ref.matmul(mx_ref.quantize(v[r]), mx_ref.quantize(np.concatenate([cols(M[q], entries(sm[q])[r * CM:r * CM + CM]) for q in range(N)], axis=1)))
        k = entries(nl[r]).reshape(T, 4)
        z = np.where(k >= 0, P[:, k], np.float32(-np.inf)).max(axis=2)
        y[r] = np.where((k >= 0).any(axis=1), z, np.float32(0))
    return {"y": y}

from concourse.mybir import dt, AluOpType, ActivationFunctionType
from concourse.bass import IndirectOffsetOnAxis

N, NT, E, CN, CM = 4, 256, 512, 128, 144
NH = NT + N * CN
XO = 16
WO = 8
NA = 64
ALU, ACT = AluOpType, ActivationFunctionType
OWN = "ssssssss"
LATE = ["ssssssss", "ssssssss", "vvssvvss"]

SCRATCH = {
    "xb": ("sbuf", [128, XO + 4 * NT], "bfloat16"),
    "eb": ("sbuf", [128, XO + 4 * E], "bfloat16"),
    "wab": ("sbuf", [128, 2048], "bfloat16"),
    "wbb": ("sbuf", [128, 2048], "bfloat16"),
    "vb": ("sbuf", [128, 512], "bfloat16"),
    "ht": ("sbuf", [128, 4 * 3 * CN], "bfloat16"),
    "mt": ("sbuf", [128, 4 * N * CM], "bfloat16"),
    "pa": ("sbuf", [128, 4 * NH], "float32"),
    "pb": ("sbuf", [128, 4 * NH], "float32"),
    "nld": ("dram", [4, 256], "int32"),
    "ps": ("psum", [128, 4096], "float32"),
}
for _n, _w in (("snl", 32), ("sml", 36), ("eds", 64), ("nlr", 256), ("pi", 1), ("b4i", 1), ("i4i", 1), ("ci", 144), ("co", 288)):
    SCRATCH[_n] = ("sbuf", [128, _w], "int32")
for _n, _w in (("pk1", 32), ("pk2", 32), ("pk", 32), ("pkt", 32), ("prow", 512), ("wn", 512), ("b4f", 1), ("ic", 1), ("ipk", 1),
               ("jm", 576), ("kk", 512), ("mask", 576), ("carry", 576), ("mv", 576), ("sc", 576), ("mv2", 576), ("sc2", 576),
               ("nmv", 256), ("nsc", 256), ("nt1", 32), ("nt2", 16), ("nt3", 16), ("nt4", 16), ("win", WO + N * CM),
               ("g0", NT), ("m1", NT), ("m2", NT), ("yb", NT)):
    SCRATCH[_n] = ("sbuf", [128, _w], "float32")
for _n, _w in (("smo", 36), ("oe", 144), ("oab", 288), ("onl", 64), ("oft0", 32), ("oft1", 32), ("oft2", 32), ("oft3", 32)):
    SCRATCH[_n] = ("sbuf", [128, _w], "uint16")
for _k in range(4):
    for _n in ("gb", "uu", "zz"):
        SCRATCH["%s%d" % (_n, _k)] = ("sbuf", [128, 4 * CM], "float32")
for _n, _w in (("h", 3 * CN), ("nn", N * CN), ("xx", NT), ("wa", 512), ("wb", 512), ("vv", 128), ("mm", N * CM), ("rr", N * CM)):
    SCRATCH[_n + "q"] = ("sbuf", [128, _w], "float8_e4m3fn_x4")
    SCRATCH[_n + "p"] = ("sbuf", [128, _w], "uint8")

SEMAPHORES = ["cv", "cs", "ct", "cg", "d_ed", "d_sn", "d_x", "d_wa", "d_wb", "d_sm", "d_nl", "d_pr", "d_e", "d_v", "d_g", "d_y",
              "lno", "lme", "go"] + ["an%d" % _k for _k in range(4)] + ["am%d" % _k for _k in range(4)]


def rank_program(g, core, T, topo):
    r = T.rank_of(core)
    if r is None:
        return
    S = T.sem
    Q = {"g": g, "v": g.vector, "s": g.scalar, "t": g.tensor, "y": g.sync}
    CS = {"v": "cv", "s": "cs", "t": "ct", "g": "cg"}
    V, A, PE = g.vector, g.scalar, g.tensor
    seen, cnt = {}, {}

    def need(q, *toks):
        best = {}
        for k, n in toks:
            best[k] = max(best.get(k, 0), n)
        for k in best:
            if seen.get((q, k), 0) < best[k]:
                Q[q].wait_ge(S[k], best[k])
                seen[(q, k)] = best[k]

    def did(q, ins):
        k = CS[q]
        cnt[k] = cnt.get(k, 0) + 1
        ins.then_inc(S[k], 1)
        return (k, cnt[k])

    def dma(q, sem, out, in_):
        Q[q].dma_start(out, in_).then_inc(S[sem], 16)
        cnt[sem] = cnt.get(sem, 0) + 16

    def tok(sem):
        return (sem, cnt[sem])

    def ts(out, in0, s1, op, s2=None, op2=None):
        if op2 is None:
            return did("v", V.tensor_scalar(out, in0, s1, None, op))
        return did("v", V.tensor_scalar(out, in0, s1, s2, op, op2))

    def tt(out, in0, in1, op):
        return did("v", V.tensor_tensor(out, in0, in1, op))

    def copy(q, out, in_):
        return did(q, V.tensor_copy(out, in_) if q == "v" else A.activation(out, in_, ACT.Copy))

    def near(d):
        a, b = topo.chip(core), topo.chip(T.cores[d])
        return 2 if topo.mates(a, b) else 1 if topo.same_plane(a, b) else 0
    others = sorted([d for d in range(N) if d != r], key=near)
    blocks = others + [r]

    def send(d, lsem, pairs, rsem):
        dst = T.cores[d]
        rid, pid, _ = topo.addr(dst)
        for o, i in pairs:
            g.remote_dma(o, i, S[rsem], S[lsem], pid, rid, topo.mask(core, dst))
            cnt[lsem] = cnt.get(lsem, 0) + len(topo.engines(core, dst))

    def arrived(s):
        return 2 * len(topo.engines(T.cores[s], core))

    dma("y", "d_ed", T.eds[0:16, 0:32], T.es[:, :])
    dma("y", "d_ed", T.eds[0:16, 32:64], T.ed[:, :])
    for k in range(8):
        dma("y" if k < 3 else "s", "d_sn", T.snl[16 * k:16 * k + 16, :], T.sn[:, :])
    dma("y", "d_x", T.xb[:, XO:XO + 512], T.x[:, 0:512])
    dma("s", "d_x", T.xb[:, XO + 512:XO + 1024], T.x[:, 512:1024])
    dma("s", "d_wa", T.wab[:, :], T.wa[:, :])
    for k in range(8):
        dma("y", "d_sm", T.sml[16 * k:16 * k + 16, :], T.sm[:, :])

    k_pi = did("g", g.iota(T.pi[:, :], [[0, 1]], 0, 1))
    k_jm = did("g", g.iota(T.jm[:, :], [[0, 144], [1, 4]], 0, 0, allow_small_or_imprecise_dtypes=True))
    k_kk = did("g", g.iota(T.kk[:, :], [[1, 512]], 0, 0, allow_small_or_imprecise_dtypes=True))
    did("v", V.memset(T.pk[0:32, :], 0.0))
    k_c = did("v", V.memset(T.carry[:, :], 1.0))
    k_xb = did("v", V.memset(T.xb[:, 0:XO], 0.0))
    k_eb = did("v", V.memset(T.eb[:, 0:XO], 0.0))
    did("v", V.memset(T.win[:, 0:WO - 1], 0.0))
    k_win = did("v", V.memset(T.win[:, WO - 1:WO], -1e29))
    need("v", k_c)
    k_c = did("v", V.memset(T.carry[:, 0:576:4], 0.0))
    need("v", k_pi)
    ts(T.b4i[:, :], T.pi[:, :], 2, ALU.logical_shift_right, 3, ALU.bitwise_and)
    k_i4 = ts(T.i4i[:, :], T.pi[:, :], 3, ALU.bitwise_and)
    need("v", k_i4)
    k_bf = copy("v", T.b4f[:, :], T.b4i[:, :])
    k_ic = ts(T.ic[:, :], T.i4i[:, :], float(XO), ALU.add)
    k_ip = ts(T.ipk[:, :], T.i4i[:, :], 4097.0, ALU.mult)
    need("v", k_jm, k_bf)
    k_mask = ts(T.mask[:, :], T.jm[:, :], T.b4f[:, 0:1], ALU.is_equal)
    hole = 4 * (NT + CN * r)
    need("s", k_c)
    did("s", A.activation(T.pa[:, hole:hole + 4 * CN], T.carry[:, 0:512], ACT.Copy, scale=0.0))
    k_hole = did("s", A.activation(T.pb[:, hole:hole + 4 * CN], T.carry[:, 0:512], ACT.Copy, scale=0.0))

    need("v", tok("d_ed"))
    ts(T.pk1[0:16, :], T.eds[0:16, 0:32], 4.0, ALU.mult)
    k = ts(T.pk2[0:16, :], T.eds[0:16, 32:64], 16384.0, ALU.mult)
    need("v", tok("d_sn"))
    k_of = {}
    for t in (2, 3, 0, 1):
        k_of[t] = ts(T["oft%d" % t][:, :], T.snl[:, :], 4.0, ALU.mult, float(XO + t), ALU.add)
    need("v", k)
    k = tt(T.pk[0:16, :], T.pk1[0:16, :], T.pk2[0:16, :], ALU.add)
    need("v", k)
    k_pkt = did("v", V.transpose(T.pkt[0:32, :], T.pk[0:32, :]))
    need("y", k_pkt)
    dma("y", "d_pr", T.prow[0:1, :], T.pkt[0:32, 0:16])
    dma("y", "d_wb", T.wbb[:, :], T.wb[:, :])
    dma("y", "d_nl", T.nld[:, :], T.nl[:, :])

    need("v", tok("d_x"), k_xb)
    need("s", tok("d_x"), k_xb)
    for o, d in enumerate(others):
        ks = []
        for q, t in (("v", 0), ("v", 1), ("s", 2), ("s", 3)):
            need(q, k_of[t])
            ks.append(copy(q, T.ht[:, 512 * o + t:512 * o + 512:4], T.xb[:, :].indirect(T["oft%d" % t][:, 8 * d:8 * d + 8])))
        need("v", *ks)
        here, there = slice(CN * o, CN * o + CN), slice(CN * r, CN * r + CN)
        k = did("v", V.quantize_mx(T.hq[:, here], T.hp[:, here], T.ht[:, 512 * o:512 * o + 512]))
        need("g", k)
        send(d, "lno", [(T.nnq[:, there].bitcast(dt.uint8), T.hq[:, here].bitcast(dt.uint8)), (T.nnp[:, there], T.hp[:, here])], "an%d" % r)
    g.sem_inc(S.go, 1)
    cnt["go"] = 1
    need("y", tok("go"))
    dma("y", "d_e", T.eb[:, XO:XO + 4 * E], T.e[:, :])
    dma("y", "d_v", T.vb[:, :], T.v[:, :])
    need("g", tok("d_pr"))
    k_wn = did("g", g.partition_broadcast(T.wn[:, :], T.prow[0:1, :], 128))
    need("g", tok("d_nl"), k_i4)
    g.indirect_dma_start(T.nlr[:, :], None, T.nld[:, :], IndirectOffsetOnAxis(ap=T.i4i[:, 0:1], axis=0), bounds_check=3).then_inc(S.d_g, 16)
    cnt["d_g"] = 16

    need("v", tok("d_wa"))
    k_wq = did("v", V.quantize_mx(T.waq[:, :], T.wap[:, :], T.wab[:, :]))
    k_xq = did("v", V.quantize_mx(T.xxq[:, :], T.xxp[:, :], T.xb[:, XO:XO + 1024]))
    need("v", tok("d_wb"))
    k_uq = did("v", V.quantize_mx(T.wbq[:, :], T.wbp[:, :], T.wbb[:, :]))

    bank = [None] * 8
    k_pw = []

    def products(cq, cp, n, who):
        ks = {}
        for j in who:
            c, p = (T.waq, T.wap) if j < 4 else (T.wbq, T.wbp)
            b = slice(128 * (j % 4), 128 * (j % 4) + 128)
            need("t", k_wq if j < 4 else k_uq)
            if bank[j]:
                need("t", bank[j])
            ks[j] = did("t", PE.matmul_mx(T.ps[:, 512 * j:512 * j + n], c[:, b], p[:, b], cq, cp, True, True))
        return ks

    def take(q, plan, h, n, ks):
        for j in ks:
            if plan[j] == q:
                need(q, ks[j])
                bank[j] = copy(q, (T.pa if j < 4 else T.pb)[:, 4 * h + j % 4:4 * h + 4 * n:4], T.ps[:, 512 * j:512 * j + n])
                k_pw.append(bank[j])

    need("t", k_xq)
    own = (OWN, 0, NT, products(T.xxq[:, :], T.xxp[:, :], NT, range(8)))
    take("s", *own)

    need("v", tok("d_sm"))
    k_smo = ts(T.smo[:, :], T.sml[:, :], 0.0, ALU.max)
    need("v", k_smo, k_kk, k_mask)
    k = tt(T.mv2[:, :], T.kk[:, :].indirect(T.smo[:, :]), T.mask[:, :], ALU.mult)
    need("v", k, k_c)
    k = did("v", V.tensor_tensor_scan(T.sc2[:, :], T.carry[:, :], T.mv2[:, :], 0.0, ALU.mult, ALU.add))
    take("v", *own)
    need("v", k, k_ic)
    k_oe = ts(T.oe[:, :], T.sc2[:, 3:576:4], 4.0, ALU.mult, T.ic[:, 0:1], ALU.add)

    def late(o):
        s = others[o]
        b = slice(CN * s, CN * s + CN)
        need("t", ("an%d" % s, arrived(s)))
        return LATE[o], NT + CN * s, CN, products(T.nnq[:, b], T.nnp[:, b], CN, (4, 5, 6, 7, 0, 1, 2, 3))

    la = late(0)
    take("s", *la)
    need("v", k_wn)
    k = tt(T.mv[:, :], T.wn[:, :].indirect(T.smo[:, :]), T.mask[:, :], ALU.mult)
    need("v", k)
    k = did("v", V.tensor_tensor_scan(T.sc[:, :], T.carry[:, :], T.mv[:, :], 0.0, ALU.mult, ALU.add))
    take("v", *la)
    need("v", k, k_ip)
    k = ts(T.ci[:, :], T.sc[:, 3:576:4], T.ipk[:, 0:1], ALU.add)
    lb = late(1)
    take("s", *lb)
    need("v", k)
    kh = ts(T.co[:, 144:288], T.ci[:, :], 12, ALU.logical_shift_right)
    kl = ts(T.co[:, 0:144], T.ci[:, :], 4095, ALU.bitwise_and)
    take("v", *lb)
    need("v", kh)
    k_ob = copy("v", T.oab[:, 144:288], T.co[:, 144:288])
    need("v", kl)
    k_oa = copy("v", T.oab[:, 0:144], T.co[:, 0:144])
    lc = late(2)
    take("v", *lc)
    take("s", *lc)

    W, H = 4 * CM, 2 * CM
    gb, uu, zz = ([T["%s%d" % (n, o)] for o in range(4)] for n in ("gb", "uu", "zz"))
    k_gb, k_u, k_z, k_r, k_q = {}, {}, {}, {}, {}

    def list_of(t, base, o, a=0, n=36):
        c = base + 36 * blocks[o] + a
        return t[:, c:c + n]

    def gather_b(q, o, a=0, b=W):
        need(q, *k_pw, k_hole, k_ob)
        k_gb.setdefault(o, []).append(copy(q, gb[o][:, a:b], T.pb[:, :].indirect(list_of(T.oab, 144, o, a // 16, (b - a) // 16))))

    def add_a(o):
        need("v", *k_pw, k_hole, k_oa, *k_gb[o])
        k_u[o] = tt(uu[o][:, :], T.pa[:, :].indirect(list_of(T.oab, 0, o)), gb[o][:, :], ALU.add)

    def add_e(o):
        need("v", tok("d_e"), k_eb, k_oe, k_u[o])
        k_z[o] = tt(zz[o][:, :], T.eb[:, :].indirect(list_of(T.oe, 0, o)), uu[o][:, :], ALU.add)

    def relu(q, o, a, b):
        need(q, k_z[o])
        out = T.mt[:, W * o + a:W * o + b]
        if q == "s":
            k = did("s", A.activation(out, zz[o][:, a:b], ACT.Relu, scale=0.05))
        else:
            k = ts(out, zz[o][:, a:b], 0.0, ALU.max, 0.05, ALU.mult)
        k_r.setdefault(o, []).append(k)

    def quant(o):
        need("v", *k_r[o])
        here, there = slice(CM * o, CM * o + CM), slice(CM * r, CM * r + CM)
        k_q[o] = did("v", V.quantize_mx(T.mmq[:, here], T.mmp[:, here], T.mt[:, W * o:W * o + W]))
        if blocks[o] != r:
            need("g", k_q[o])
            send(blocks[o], "lme", [(T.rrq[:, there].bitcast(dt.uint8), T.mmq[:, here].bitcast(dt.uint8)), (T.rrp[:, there], T.mmp[:, here])], "am%d" % r)

    gather_b("s", 0, 0, H)
    gather_b("v", 0, H, W)
    gather_b("s", 1)
    gather_b("s", 2)
    add_a(0)
    add_e(0)
    relu("s", 0, 0, W)
    add_a(1)
    gather_b("s", 3)
    add_e(1)
    quant(0)
    relu("s", 1, 0, W)
    add_a(2)
    quant(1)
    add_e(2)
    relu("s", 2, 0, H)
    relu("v", 2, H, W)
    quant(2)
    add_a(3)
    need("v", tok("d_g"))
    k = tt(T.nmv[:, :], T.nlr[:, :], T.mask[:, 0:256], ALU.mult)
    need("v", tok("d_v"))
    k_vq = did("v", V.quantize_mx(T.vvq[:, :], T.vvp[:, :], T.vb[:, :]))
    add_e(3)
    need("v", k)
    k = did("v", V.tensor_tensor_scan(T.nsc[:, :], T.carry[:, 0:256], T.nmv[:, :], 0.0, ALU.mult, ALU.add))
    relu("s", 3, 0, H)
    relu("v", 3, H, W)
    need("v", k)
    k = tt(T.nt1[:, :], T.nsc[:, 3:128:4], T.nsc[:, 131:256:4], ALU.max)
    quant(3)
    need("v", k)
    k = tt(T.nt2[:, :], T.nt1[:, 0:16], T.nt1[:, 16:32], ALU.max)
    ts(T.onl[:, 16:64], T.nsc[:, 67:256:4], float(WO), ALU.add)
    need("v", k)
    k = ts(T.nt3[:, :], T.nt2[:, :], 0.0, ALU.is_lt)
    need("v", k)
    k = tt(T.nt4[:, :], T.nsc[:, 3:64:4], T.nt3[:, :], ALU.subtract)
    need("v", k)
    k_onl = ts(T.onl[:, 0:16], T.nt4[:, :], float(WO), ALU.add)

    need("t", k_vq)
    k_w = []
    for n, o in enumerate((0, 3, 1, 2)):
        s = blocks[o]
        if s == r:
            need("t", k_q[o])
            cq, cp = T.mmq[:, CM * o:CM * o + CM], T.mmp[:, CM * o:CM * o + CM]
        else:
            need("t", ("am%d" % s, arrived(s)))
            cq, cp = T.rrq[:, CM * s:CM * s + CM], T.rrp[:, CM * s:CM * s + CM]
        need("t", bank[n])
        k = did("t", PE.matmul_mx(T.ps[:, 512 * n:512 * n + CM], T.vvq[:, :], T.vvp[:, :], cq, cp, True, True))
        need("s", k)
        k_w.append(copy("s", T.win[:, WO + CM * s:WO + CM * s + CM], T.ps[:, 512 * n:512 * n + CM]))

    def at(f, a, b):
        return T.win[:, :].indirect(T.onl[:, 16 * f + a // 16:16 * f + b // 16])

    def largest(f, a, b, k):
        i, o = (None, (T.g0, T.m1), (T.m1, T.m2), (T.m2, T.yb))[f]
        need("v", k)
        return tt(o[:, a:b], at(f, a, b), i[:, a:b], ALU.max)

    need("s", k_onl, k_win, *k_w)
    need("v", k_onl, k_win, *k_w)
    kb = copy("s", T.g0[:, NA:NT], at(0, NA, NT))
    ka = copy("v", T.g0[:, 0:NA], at(0, 0, NA))
    ka = largest(1, 0, NA, ka)
    ka = largest(2, 0, NA, ka)
    kb = largest(1, NA, NT, kb)
    ka = largest(3, 0, NA, ka)
    kb = largest(2, NA, NT, kb)
    kb = largest(3, NA, NT, kb)
    need("y", ka)
    dma("y", "d_y", T.y[:, 0:NA], T.yb[:, 0:NA])
    need("y", kb)
    dma("y", "d_y", T.y[:, NA:NT], T.yb[:, NA:NT])

    for k in cnt:
        need("g", tok(k))
    for s in others:
        need("g", ("an%d" % s, arrived(s)), ("am%d" % s, arrived(s)))
